import numpy as np
import ml_dtypes


def mxq(x, axis, fmt="e4m3"):
    dtype, down = {"e4m3": (ml_dtypes.float8_e4m3fn, 7), "e5m2": (ml_dtypes.float8_e5m2, 14)}[fmt]
    v = np.moveaxis(np.asarray(x, np.float32).astype(ml_dtypes.bfloat16).astype(np.float64), axis, -1)
    blocks = v.reshape(v.shape[:-1] + (-1, 32))
    amax = np.abs(blocks).max(-1, keepdims=True)
    byte = np.maximum(np.where(amax > 0, np.frexp(amax)[1] - 1 + 127, 0) - down, 1)
    scale = np.exp2(byte - 127.0)
    codes = (blocks / scale).astype(np.float32).astype(dtype).astype(np.float64)
    return np.moveaxis((codes * scale).reshape(v.shape), -1, axis)


WIDE = False


def mx_kscale(k):
    if not WIDE:
        return np.ones(k)
    levels = np.array([10, -10, 5, -5, 0])
    if k % 512:
        return np.exp2(np.random.permutation(np.resize(levels, k // 32))).repeat(32)
    a = np.empty((k // 512, 16))
    for p in range(k // 512):
        a[p, :8] = np.random.permutation(np.resize(levels, 8))
        for g in range(8):
            far = levels[np.abs(levels - a[p, g]) >= 10]
            a[p, g + 8] = far[np.random.randint(len(far))]
    return np.exp2(a.ravel()).repeat(32)


BF16 = ml_dtypes.bfloat16


def bf(x):
    return np.asarray(x, np.float32).astype(BF16)


def f64(x):
    return np.asarray(x).astype(np.float64)

def planes(Y):
    n, m = Y.shape
    b = f64(bf(Y)).reshape(n // 32, 32, m)
    amax = np.abs(b).max(1)
    byte = np.clip(np.where(amax > 0, np.frexp(amax)[1] - 1 + 127 - 7, 1), 1, 254)
    codes = (b * np.exp2(127.0 - byte)[:, None, :]).reshape(n, m).astype(np.float32).astype(ml_dtypes.float8_e4m3fn).view(np.uint8)
    words = codes.reshape(n // 512, 128, 4, m).transpose(0, 1, 3, 2)
    return np.ascontiguousarray(words), np.ascontiguousarray(byte.astype(np.uint8).reshape(n // 512, 16, m))


NX, NY = 1024, 1536


def setup_inputs():
    s = mx_kscale(NX)
    t = mx_kscale(NY)
    rhs = np.random.randn(NY, NX) * s[None, :]
    left = np.random.randn(NX, NX) / np.sqrt(NX) / s[:, None]
    row_scale = np.exp(0.3 * np.random.randn(NY)) * t
    right = np.random.randn(NY, NY) / np.sqrt(NY) / t[:, None]
    lam = 0.2 + 0.5 * np.exp(0.8 * np.random.randn(NX))
    mu = 0.1 + 0.2 * np.exp(0.5 * np.random.randn(NY))
    return {"rhs": bf(rhs), "left": bf(left), "row_scale": bf(row_scale),
            "right": bf(right), "lam": bf(lam), "mu": bf(mu)}

def reference(rhs, left, row_scale, right, lam, mu):
    p = mxq(f64(rhs), 1, "e4m3") @ mxq(f64(left), 0, "e4m3")
    h = p * f64(row_scale)[:, None]
    z = mxq(h, 0, "e4m3").T @ mxq(f64(right), 0, "e4m3")
    y = z / (f64(lam)[:, None] + f64(mu)[None, :])
    Y = y
    words, scales = planes(Y)
    return y, words, scales

@@ -1,0 +1,421 @@
+from contextlib import ExitStack
+
+import concourse.mybir as mybir
+from concourse.masks import make_identity
+
+NX, NY = 1024, 1536
+FLOPS = 2 * NY * NX * NX + 2 * NX * NY * NY
+
+F32 = mybir.dt.float32
+BF16 = mybir.dt.bfloat16
+I32 = mybir.dt.int32
+U32 = mybir.dt.uint32
+U8 = mybir.dt.uint8
+FP8X4 = mybir.dt.float8_e4m3fn_x4
+ACT = mybir.ActivationFunctionType
+ALU = mybir.AluOpType
+
+P = 128
+PACK = 4
+KP = P * PACK
+W = 512
+I_PASSES = NX // KP
+J_PASSES = NY // KP
+A_GROUPS = NX // KP
+L_CHUNKS = NY // W
+MU_COLS = NY // P
+STAGE_BUFS = 8
+WEIGHT_BUFS = 4
+Y_BUFS = 4
+
+
+def tile_sylvester_eigen_coordinates_h3_kernel(
+    tc, rhs, left, row_scale, right, lam, mu, out_0, out_1, out_2
+):
+    nc = tc.nc
+    with ExitStack() as ctx:
+        keep = ctx.enter_context(tc.tile_pool(name="keep", bufs=1))
+        ring = ctx.enter_context(tc.tile_pool(name="ring", bufs=1))
+        shared = ctx.enter_context(tc.tile_pool(name="shared", bufs=1))
+        psum = ctx.enter_context(tc.psum_pool(name="psum", bufs=8))
+        ctx.enter_context(tc.manual_schedule())
+
+        raw = {}
+        staged = {}
+        banks = {}
+        codes = {}
+        scales = {}
+        weight = {}
+        y32 = {}
+
+        def new_bank(key):
+            banks[key] = psum.tile([P, W], F32, name="bank", tag="bank")
+            return banks[key]
+
+        def copy_on(engine, out, in_):
+            if engine == "V":
+                nc.vector.tensor_copy(out=out, in_=in_)
+            else:
+                nc.scalar.copy(out=out, in_=in_)
+
+        def load_rows(key, src, width):
+            raw[key] = keep.tile([P, PACK, width], BF16, name="raw_%s_%d_%d" % key)
+            nc.sync.dma_start(out=raw[key][:], in_=src.rearrange("(p t) w -> p t w", t=PACK))
+
+        def load_left(c, g):
+            load_rows(("left", c, g), left[c * KP : (c + 1) * KP, g * W : (g + 1) * W], W)
+
+        def load_right_first(c):
+            load_rows(("right", c, 0), right[c * KP : (c + 1) * KP, 0:W], W)
+
+        def load_right_rest(c):
+            load_rows(("right", c, 1), right[c * KP : (c + 1) * KP, W:NY], NY - W)
+
+        def load_rhs(jg, tp):
+            raw["rhs", jg, tp] = shared.tile([P, 2, NX], BF16, name="rhs_raw", tag="rhs_raw", bufs=6, offset=0)
+            rows = rhs[jg * KP : (jg + 1) * KP, :].rearrange("(m t) i -> m t i", t=PACK)
+            nc.sync.dma_start(out=raw["rhs", jg, tp][:], in_=rows[:, 2 * tp : 2 * tp + 2, :])
+
+        def new_stage(key):
+            staged[key] = ring.tile([P, W, PACK], BF16, name="stage", tag="stage", bufs=STAGE_BUFS, align_bytes=64)
+            return staged[key]
+
+        def interleave(engine, dst, src):
+            copy_on(
+                engine,
+                dst.rearrange("p (c i) t -> p c t i", i=4),
+                src.rearrange("p t (c i) -> p c t i", i=4),
+            )
+
+        def interleave_left(engine, c, g):
+            interleave(engine, new_stage(("left", c, g))[:], raw["left", c, g][:])
+
+        def interleave_right(engine, c, lc):
+            if lc == 0:
+                src = raw["right", c, 0][:]
+            else:
+                src = raw["right", c, 1][:, :, (lc - 1) * W : lc * W]
+            interleave(engine, new_stage(("right", c, lc))[:], src)
+
+        def quantize(key):
+            codes[key] = keep.tile([P, W], U32, name="codes_%s_%d_%d" % key, align_bytes=64)
+            scales[key] = keep.tile([P, W], U8, name="scales_%s_%d_%d" % key, align_bytes=64)
+            nc.vector.quantize_mx(
+                out=codes[key][:].bitcast(FP8X4),
+                scales=scales[key][:],
+                in_=staged[key][:].rearrange("p w t -> p (w t)"),
+            )
+
+        def transpose_rhs(jg, c, tp):
+            bank = new_bank(("rhs", jg, c, tp))
+            for t2 in range(2):
+                words = raw["rhs", jg, tp][:, t2, :].bitcast(F32)
+                for u in range(2):
+                    q = 2 * t2 + u
+                    nc.tensor.transpose(
+                        bank[:, q * P : (q + 1) * P], words[:, 256 * c + u : 256 * (c + 1) : 2], ident[:]
+                    )
+
+        def copy_rhs(engine, jg, c, tp):
+            if tp == 0:
+                new_stage(("rhs", jg, c))
+            dst = staged["rhs", jg, c][:, tp * 2 * P : (tp + 1) * 2 * P, :].rearrange("p w t -> p (w t)").bitcast(F32)
+            copy_on(
+                engine,
+                dst.rearrange("p (t m u) -> p t m u", t=2, u=2),
+                banks["rhs", jg, c, tp][:].rearrange("p (t u m) -> p t m u", t=2, u=2),
+            )
+
+        def mx_pass(out, stat, stat_cols, mov, mov_cols, start, stop):
+            nc.tensor.matmul_mx(
+                out=out,
+                lhsT=codes[stat][:, stat_cols].bitcast(FP8X4),
+                lhsT_scale=scales[stat][:, stat_cols],
+                rhs=codes[mov][:, mov_cols].bitcast(FP8X4),
+                rhs_scale=scales[mov][:, mov_cols],
+                start=start,
+                stop=stop,
+            )
+
+        def product_p(g, jg, b):
+            bank = new_bank(("p", g, jg, b))
+            for t in range(PACK):
+                for c in range(I_PASSES):
+                    mx_pass(
+                        bank[:, t * P : (t + 1) * P],
+                        ("rhs", jg, c), slice(t * P, (t + 1) * P),
+                        ("left", c, g), slice(b * P, (b + 1) * P),
+                        c == 0, c == I_PASSES - 1,
+                    )
+
+        def scale_rows(g, jg, b):
+            if b == 0:
+                new_stage(("h", jg, g))
+            dst = staged["h", jg, g][:].rearrange("p (s m) t -> p s m t", s=PACK)[:, :, 32 * b : 32 * (b + 1), :]
+            nc.vector.tensor_tensor(
+                out=dst,
+                in0=banks["p", g, jg, b][:].rearrange("p (t m s) -> p s m t", t=PACK, s=PACK),
+                in1=rs[:, jg : jg + 1, :].unsqueeze(1).to_broadcast([P, PACK, 32, PACK]),
+                op=ALU.mult,
+            )
+
+        def product_z(g, lc, s):
+            bank = new_bank(("z", g, lc, s))
+            for c in range(J_PASSES):
+                mx_pass(
+                    bank[:], ("h", c, g), slice(s * P, (s + 1) * P), ("right", c, lc), slice(0, W),
+                    c == 0, c == J_PASSES - 1,
+                )
+
+        def sigmoid_weight(g, lc, s):
+            if s == 0:
+                weight[g, lc] = ring.tile([P, PACK, W], F32, name="weight", tag="weight", bufs=WEIGHT_BUFS)
+            nc.scalar.activation(
+                out=weight[g, lc][:, s, :],
+                in_=ln_mu_rows[lc][:],
+                func=ACT.Sigmoid,
+                bias=ln_lam[:, PACK * g + s : PACK * g + s + 1],
+                scale=-1.0,
+            )
+
+        def divide(g, lc, s):
+            if s == 0:
+                y32[g, lc] = shared.tile([P, PACK, W], F32, name="y32", tag="y32", bufs=Y_BUFS, offset=0)
+            nc.vector.scalar_tensor_tensor(
+                out=y32[g, lc][:, s, :],
+                in0=banks["z", g, lc, s][:],
+                scalar=inv_lam[:, PACK * g + s : PACK * g + s + 1],
+                in1=weight[g, lc][:, s, :],
+                op0=ALU.mult,
+                op1=ALU.mult,
+            )
+
+        def store_y(g, lc, s0, s1):
+            rows = out_0[g * KP : (g + 1) * KP, lc * W : (lc + 1) * W].rearrange("(p s) l -> p s l", s=PACK)
+            nc.sync.dma_start(out=rows[:, s0:s1, :], in_=y32[g, lc][:, s0:s1, :])
+
+        def round_y(engine, g, lc, lo, hi):
+            if lo == 0:
+                new_stage(("y", g, lc))
+            interleave(engine, staged["y", g, lc][:, lo:hi, :], y32[g, lc][:, :, lo:hi])
+
+        def quantize_y(g, lc):
+            cols = slice(lc * W, (lc + 1) * W)
+            y_codes = ring.tile([P, W], U32, name="y_codes", tag="y_codes", bufs=6, align_bytes=64)
+            nc.vector.quantize_mx(
+                out=y_codes[:].bitcast(FP8X4),
+                scales=y_scales[PACK * g :, cols],
+                in_=staged["y", g, lc][:].rearrange("p w t -> p (w t)"),
+            )
+            dst = out_1[g].rearrange("p m t -> p (m t)").bitcast(I32)
+            nc.sync.dma_start(out=dst[:, cols], in_=y_codes[:].bitcast(I32))
+
+        def store_scales(lc0, lc1, queues):
+            cols = slice(lc0 * W, lc1 * W)
+            for q in range(4):
+                queues[q].dma_start(
+                    out=out_2[:, 4 * q : 4 * q + 4, cols].bitcast(I32),
+                    in_=y_scales[32 * q : 32 * q + 8, cols].bitcast(I32),
+                )
+
+        def spread_mu(b):
+            bank = new_bank(("mu", b))
+            for m in range(4):
+                col = 4 * b + m
+                nc.tensor.transpose(
+                    bank[:, m * P : (m + 1) * P], ln_mu[:, col : col + 1].to_broadcast([P, P]), ident[:]
+                )
+
+        def copy_mu(engine, b):
+            dst = ln_mu_all[:].rearrange("p (n m) -> p n m", m=MU_COLS)[:, :, 4 * b : 4 * b + 4]
+            copy_on(engine, dst, banks["mu", b][:].rearrange("p (m n) -> p n m", m=4))
+
+        ident = keep.tile([P, P], F32, name="ident")
+        mu_sb = keep.tile([P, MU_COLS], BF16, name="mu_sb")
+        lam_sb = keep.tile([P, A_GROUPS, PACK], BF16, name="lam_sb")
+        rs = keep.tile([P, J_PASSES, PACK], BF16, name="rs")
+        one = keep.tile([P, 1], F32, name="one")
+        warm = keep.tile([P, 2], F32, name="warm")
+        ln_mu = keep.tile([P, MU_COLS], F32, name="ln_mu")
+        ln_lam = keep.tile([P, A_GROUPS * PACK], F32, name="ln_lam")
+        inv_lam = keep.tile([P, A_GROUPS * PACK], F32, name="inv_lam")
+        ln_mu_all = keep.tile([P, NY], F32, name="ln_mu_all")
+        ln_mu_rows = [ln_mu_all[:, lc * W : (lc + 1) * W] for lc in range(L_CHUNKS)]
+        y_scales = keep.tile([P, NY], U8, name="y_scales", align_bytes=64)
+
+        nc.scalar.dma_start(out=mu_sb[:], in_=mu.rearrange("(n m) -> n m", m=MU_COLS))
+        nc.scalar.dma_start(out=lam_sb[:], in_=lam.rearrange("(g p s) -> p g s", p=P, s=PACK))
+        make_identity(nc, ident[:])
+        nc.vector.memset(one[:], 1.0)
+        nc.scalar.activation(out=warm[:, 0:1], in_=one[:], func=ACT.Ln)
+
+        load_left(0, 0)
+        load_rhs(0, 0)
+        load_rhs(0, 1)
+        load_left(1, 0)
+        nc.sync.dma_start(out=rs[:], in_=row_scale.rearrange("(g p t) -> p g t", p=P, t=PACK))
+        load_left(0, 1)
+        load_rhs(1, 0)
+        load_rhs(1, 1)
+        load_left(1, 1)
+        load_rhs(2, 0)
+        load_rhs(2, 1)
+        for c in range(J_PASSES):
+            load_right_first(c)
+        for c in range(J_PASSES):
+            load_right_rest(c)
+
+        nc.scalar.activation(out=ln_mu[:], in_=mu_sb[:], func=ACT.Ln)
+        nc.scalar.activation(out=ln_lam[:], in_=lam_sb[:].rearrange("p g s -> p (g s)"), func=ACT.Ln)
+        nc.scalar.activation(out=warm[:, 1:2], in_=one[:], func=ACT.Sigmoid)
+        nc.vector.reciprocal(out=inv_lam[:], in_=lam_sb[:].rearrange("p g s -> p (g s)"))
+
+        def rhs_half(jg, tp):
+            for c in range(I_PASSES):
+                transpose_rhs(jg, c, tp)
+            for c in range(I_PASSES):
+                copy_rhs("S", jg, c, tp)
+
+        def weights(g, lc):
+            for s in range(PACK):
+                sigmoid_weight(g, lc, s)
+
+        def stage1(g, jg, bs=range(4)):
+            for b in bs:
+                product_p(g, jg, b)
+                scale_rows(g, jg, b)
+
+        def products(g, jg):
+            for b in range(4):
+                product_p(g, jg, b)
+
+        def scale_all(g, jg, bs=range(4)):
+            for b in bs:
+                scale_rows(g, jg, b)
+
+        def products_z(g, lc):
+            for s in range(PACK):
+                product_z(g, lc, s)
+
+        def divide_all(g, lc):
+            for s in range(PACK):
+                divide(g, lc, s)
+                if s % 2:
+                    store_y(g, lc, s - 1, s + 1)
+
+        def finish(g, lc, split):
+            round_y("V", g, lc, 0, split)
+            round_y("S", g, lc, split, W)
+
+        for b in range(3):
+            spread_mu(b)
+            copy_mu("V", b)
+        interleave_left("V", 0, 0)
+        sigmoid_weight(0, 0, 0)
+        sigmoid_weight(0, 0, 1)
+        rhs_half(0, 0)
+        quantize(("left", 0, 0))
+        rhs_half(0, 1)
+        interleave_left("V", 1, 0)
+        quantize(("rhs", 0, 0))
+        quantize(("rhs", 0, 1))
+        quantize(("left", 1, 0))
+        interleave_left("V", 0, 1)
+        sigmoid_weight(0, 0, 2)
+        sigmoid_weight(0, 0, 3)
+        sigmoid_weight(0, 1, 0)
+        sigmoid_weight(0, 1, 1)
+
+        def pair(g, jg, half):
+            for b in (2 * half, 2 * half + 1):
+                product_p(g, jg, b)
+
+        pair(0, 0, 0)
+        sigmoid_weight(0, 1, 2)
+        sigmoid_weight(0, 1, 3)
+        sigmoid_weight(1, 0, 0)
+        rhs_half(1, 0)
+        pair(0, 0, 1)
+        scale_all(0, 0, (0,))
+        quantize(("left", 0, 1))
+        scale_all(0, 0, (1,))
+        interleave_left("V", 1, 1)
+        scale_all(0, 0, (2,))
+        quantize(("left", 1, 1))
+        scale_all(0, 0, (3,))
+        sigmoid_weight(1, 0, 1)
+        rhs_half(1, 1)
+        pair(1, 0, 0)
+        sigmoid_weight(1, 0, 2)
+        sigmoid_weight(1, 0, 3)
+        rhs_half(2, 0)
+        pair(1, 0, 1)
+        quantize(("rhs", 1, 0))
+        quantize(("rhs", 1, 1))
+        quantize(("h", 0, 0))
+        interleave_right("S", 0, 0)
+        scale_all(1, 0)
+        pair(0, 1, 0)
+        rhs_half(2, 1)
+        pair(0, 1, 1)
+        interleave_right("S", 1, 0)
+        scale_all(0, 1, (0,))
+        quantize(("h", 0, 1))
+        scale_all(0, 1, (1,))
+        quantize(("right", 0, 0))
+        quantize(("rhs", 2, 0))
+        quantize(("rhs", 2, 1))
+        scale_all(0, 1, (2, 3))
+        interleave_right("S", 2, 0)
+        products(0, 2)
+        quantize(("right", 1, 0))
+        quantize(("h", 1, 0))
+        interleave_right("S", 0, 1)
+        scale_all(0, 2)
+        products(1, 1)
+        quantize(("right", 2, 0))
+        quantize(("h", 2, 0))
+        interleave_right("S", 1, 1)
+        interleave_right("S", 2, 1)
+        scale_all(1, 1)
+        products_z(0, 0)
+        quantize(("right", 0, 1))
+        quantize(("h", 1, 1))
+        quantize(("right", 1, 1))
+        interleave_right("S", 0, 2)
+        divide_all(0, 0)
+        products(1, 2)
+        quantize(("right", 2, 1))
+        round_y("S", 0, 0, 0, W)
+        interleave_right("S", 1, 2)
+        scale_all(1, 2)
+        products_z(0, 1)
+        quantize(("right", 0, 2))
+        quantize(("h", 2, 1))
+        quantize_y(0, 0)
+        interleave_right("S", 2, 2)
+        divide_all(0, 1)
+        products_z(1, 0)
+        quantize(("right", 1, 2))
+        round_y("S", 0, 1, 0, W)
+        weights(1, 1)
+        divide_all(1, 0)
+        products_z(1, 1)
+        quantize(("right", 2, 2))
+        quantize_y(0, 1)
+        finish(1, 0, 256)
+        weights(0, 2)
+        divide_all(1, 1)
+        products_z(0, 2)
+        quantize_y(1, 0)
+        finish(1, 1, 256)
+        weights(1, 2)
+        divide_all(0, 2)
+        products_z(1, 2)
+        quantize_y(1, 1)
+        finish(0, 2, 128)
+        divide_all(1, 2)
+        quantize_y(0, 2)
+        finish(1, 2, 320)
+        quantize_y(1, 2)
+        store_scales(0, 3, [nc.sync, nc.scalar, nc.sync, nc.scalar])

@@ -24,9 +24,10 @@ J_PASSES = NY // KP
 A_GROUPS = NX // KP
 L_CHUNKS = NY // W
 MU_COLS = NY // P
-STAGE_BUFS = 8
-WEIGHT_BUFS = 4
+BUFS = {"stage": 6, "gstage": 1, "gstage2": 1, "sstage": 2}
+WEIGHT_BUFS = 3
 Y_BUFS = 4
+G_COLS = 256
 
 
 def tile_sylvester_eigen_coordinates_h3_kernel(
@@ -76,11 +77,16 @@ def tile_sylvester_eigen_coordinates_h3_kernel(
             rows = rhs[jg * KP : (jg + 1) * KP, :].rearrange("(m t) i -> m t i", t=PACK)
             nc.sync.dma_start(out=raw["rhs", jg, tp][:], in_=rows[:, 2 * tp : 2 * tp + 2, :])
 
-        def new_stage(key):
-            staged[key] = ring.tile([P, W, PACK], BF16, name="stage", tag="stage", bufs=STAGE_BUFS, align_bytes=64)
+        def new_stage(key, tag="stage", width=W):
+            staged[key] = ring.tile([P, width, PACK], BF16, name=tag, tag=tag, bufs=BUFS[tag], align_bytes=64)
             return staged[key]
 
         def interleave(engine, dst, src):
+            if engine == "G":
+                nc.gpsimd.tensor_scalar(
+                    out=dst, in0=src.rearrange("p t w -> p w t"), scalar1=1.0, scalar2=0.0, op0=ALU.mult, op1=ALU.add
+                )
+                return
             copy_on(
                 engine,
                 dst.rearrange("p (c i) t -> p c t i", i=4),
@@ -90,21 +96,34 @@ def tile_sylvester_eigen_coordinates_h3_kernel(
         def interleave_left(engine, c, g):
             interleave(engine, new_stage(("left", c, g))[:], raw["left", c, g][:])
 
-        def interleave_right(engine, c, lc):
+        def right_cols(c, lc):
             if lc == 0:
-                src = raw["right", c, 0][:]
+                return raw["right", c, 0][:]
+            return raw["right", c, 1][:, :, (lc - 1) * W : lc * W]
+
+        def interleave_right(engine, c, lc, tag="stage"):
+            interleave(engine, new_stage(("right", c, lc), tag)[:], right_cols(c, lc))
+
+        def interleave_shared(key, src, tag="gstage"):
+            interleave("G", new_stage(key + ("G",), tag, G_COLS)[:], src[:, :, 0:G_COLS])
+            interleave("S", new_stage(key + ("S",), "sstage", W - G_COLS)[:], src[:, :, G_COLS:W])
+
+        def quantize_into(key, codes_ap, scales_ap):
+            if key in staged:
+                parts = [(key, slice(0, W))]
             else:
-                src = raw["right", c, 1][:, :, (lc - 1) * W : lc * W]
-            interleave(engine, new_stage(("right", c, lc))[:], src)
+                parts = [(key + ("S",), slice(G_COLS, W)), (key + ("G",), slice(0, G_COLS))]
+            for part, cols in parts:
+                nc.vector.quantize_mx(
+                    out=codes_ap[:, cols].bitcast(FP8X4),
+                    scales=scales_ap[:, cols],
+                    in_=staged[part][:].rearrange("p w t -> p (w t)"),
+                )
 
         def quantize(key):
             codes[key] = keep.tile([P, W], U32, name="codes_%s_%d_%d" % key, align_bytes=64)
             scales[key] = keep.tile([P, W], U8, name="scales_%s_%d_%d" % key, align_bytes=64)
-            nc.vector.quantize_mx(
-                out=codes[key][:].bitcast(FP8X4),
-                scales=scales[key][:],
-                in_=staged[key][:].rearrange("p w t -> p (w t)"),
-            )
+            quantize_into(key, codes[key][:], scales[key][:])
 
         def transpose_rhs(jg, c, tp):
             bank = new_bank(("rhs", jg, c, tp))
@@ -117,9 +136,13 @@ def tile_sylvester_eigen_coordinates_h3_kernel(
                     )
 
         def copy_rhs(engine, jg, c, tp):
-            if tp == 0:
-                new_stage(("rhs", jg, c))
-            dst = staged["rhs", jg, c][:, tp * 2 * P : (tp + 1) * 2 * P, :].rearrange("p w t -> p (w t)").bitcast(F32)
+            if (jg, c) == (2, 1):
+                half = new_stage(("rhs", jg, c, "GS"[tp]), ("gstage", "sstage")[tp], 2 * P)[:]
+            else:
+                if tp == 0:
+                    new_stage(("rhs", jg, c))
+                half = staged["rhs", jg, c][:, tp * 2 * P : (tp + 1) * 2 * P, :]
+            dst = half.rearrange("p w t -> p (w t)").bitcast(F32)
             copy_on(
                 engine,
                 dst.rearrange("p (t m u) -> p t m u", t=2, u=2),
@@ -159,9 +182,27 @@ def tile_sylvester_eigen_coordinates_h3_kernel(
                 op=ALU.mult,
             )
 
-        def product_z(g, lc, s):
-            bank = new_bank(("z", g, lc, s))
-            for c in range(J_PASSES):
+        def product_p_wide(g, jg, t):
+            bank = new_bank(("pw", g, jg, t))
+            for c in range(I_PASSES):
+                mx_pass(
+                    bank[:], ("rhs", jg, c), slice(t * P, (t + 1) * P), ("left", c, g), slice(0, W),
+                    c == 0, c == I_PASSES - 1,
+                )
+
+        def scale_slot(g, jg, t):
+            if t == 0:
+                raw["h", jg, g] = ring.tile([P, PACK, W], BF16, name="h_rows", tag="h_rows", bufs=2)
+            nc.scalar.activation(
+                out=raw["h", jg, g][:, t, :].rearrange("p (s m) -> p s m", s=PACK),
+                in_=banks["pw", g, jg, t][:].rearrange("p (m s) -> p s m", s=PACK),
+                func=ACT.Copy,
+                scale=rs32[:, PACK * jg + t : PACK * jg + t + 1],
+            )
+
+        def product_z(g, lc, s, passes=range(J_PASSES)):
+            bank = new_bank(("z", g, lc, s)) if passes[0] == 0 else banks["z", g, lc, s]
+            for c in passes:
                 mx_pass(
                     bank[:], ("h", c, g), slice(s * P, (s + 1) * P), ("right", c, lc), slice(0, W),
                     c == 0, c == J_PASSES - 1,
@@ -195,18 +236,14 @@ def tile_sylvester_eigen_coordinates_h3_kernel(
             nc.sync.dma_start(out=rows[:, s0:s1, :], in_=y32[g, lc][:, s0:s1, :])
 
         def round_y(engine, g, lc, lo, hi):
-            if lo == 0:
+            if ("y", g, lc) not in staged:
                 new_stage(("y", g, lc))
             interleave(engine, staged["y", g, lc][:, lo:hi, :], y32[g, lc][:, :, lo:hi])
 
         def quantize_y(g, lc):
             cols = slice(lc * W, (lc + 1) * W)
             y_codes = ring.tile([P, W], U32, name="y_codes", tag="y_codes", bufs=6, align_bytes=64)
-            nc.vector.quantize_mx(
-                out=y_codes[:].bitcast(FP8X4),
-                scales=y_scales[PACK * g :, cols],
-                in_=staged["y", g, lc][:].rearrange("p w t -> p (w t)"),
-            )
+            quantize_into(("y", g, lc), y_codes[:], y_scales[PACK * g :, cols])
             dst = out_1[g].rearrange("p m t -> p (m t)").bitcast(I32)
             nc.sync.dma_start(out=dst[:, cols], in_=y_codes[:].bitcast(I32))
 
@@ -234,6 +271,7 @@ def tile_sylvester_eigen_coordinates_h3_kernel(
         mu_sb = keep.tile([P, MU_COLS], BF16, name="mu_sb")
         lam_sb = keep.tile([P, A_GROUPS, PACK], BF16, name="lam_sb")
         rs = keep.tile([P, J_PASSES, PACK], BF16, name="rs")
+        rs32 = keep.tile([P, J_PASSES * PACK], F32, name="rs32")
         one = keep.tile([P, 1], F32, name="one")
         warm = keep.tile([P, 2], F32, name="warm")
         ln_mu = keep.tile([P, MU_COLS], F32, name="ln_mu")
@@ -254,9 +292,9 @@ def tile_sylvester_eigen_coordinates_h3_kernel(
         load_rhs(0, 1)
         load_left(1, 0)
         nc.sync.dma_start(out=rs[:], in_=row_scale.rearrange("(g p t) -> p g t", p=P, t=PACK))
-        load_left(0, 1)
         load_rhs(1, 0)
         load_rhs(1, 1)
+        load_left(0, 1)
         load_left(1, 1)
         load_rhs(2, 0)
         load_rhs(2, 1)
@@ -307,6 +345,37 @@ def tile_sylvester_eigen_coordinates_h3_kernel(
             round_y("V", g, lc, 0, split)
             round_y("S", g, lc, split, W)
 
+        def pair(g, jg, half):
+            for b in (2 * half, 2 * half + 1):
+                product_p(g, jg, b)
+
+        def shared_right(c, lc):
+            interleave_shared(("right", c, lc), right_cols(c, lc))
+
+        def shared_y(g, lc):
+            interleave_shared(("y", g, lc), y32[g, lc][:])
+
+        def wide(g, jg):
+            for t in range(PACK):
+                product_p_wide(g, jg, t)
+
+        def scale_wide(g, jg):
+            for t in range(PACK):
+                scale_slot(g, jg, t)
+
+        def z_passes(g, lc, passes):
+            for c in passes:
+                for s in range(PACK):
+                    product_z(g, lc, s, range(c, c + 1))
+
+        def whole(engine, key, src):
+            interleave(engine, new_stage(key, "gstage" if engine == "G" else "stage")[:], src)
+
+        def warm_up(n):
+            bank = new_bank("warm")
+            for k in range(n):
+                mx_pass(bank[:], ("left", 0, 0), slice(0, P), ("left", 0, 0), slice(0, W), True, True)
+
         for b in range(3):
             spread_mu(b)
             copy_mu("V", b)
@@ -320,100 +389,97 @@ def tile_sylvester_eigen_coordinates_h3_kernel(
         quantize(("rhs", 0, 0))
         quantize(("rhs", 0, 1))
         quantize(("left", 1, 0))
-        interleave_left("V", 0, 1)
+        nc.vector.tensor_copy(out=rs32[:], in_=rs[:].rearrange("p g t -> p (g t)"))
         sigmoid_weight(0, 0, 2)
         sigmoid_weight(0, 0, 3)
         sigmoid_weight(0, 1, 0)
         sigmoid_weight(0, 1, 1)
-
-        def pair(g, jg, half):
-            for b in (2 * half, 2 * half + 1):
-                product_p(g, jg, b)
-
+        warm_up(3)
+        rhs_half(1, 0)
         pair(0, 0, 0)
         sigmoid_weight(0, 1, 2)
         sigmoid_weight(0, 1, 3)
-        sigmoid_weight(1, 0, 0)
-        rhs_half(1, 0)
-        pair(0, 0, 1)
-        scale_all(0, 0, (0,))
-        quantize(("left", 0, 1))
-        scale_all(0, 0, (1,))
-        interleave_left("V", 1, 1)
-        scale_all(0, 0, (2,))
-        quantize(("left", 1, 1))
-        scale_all(0, 0, (3,))
-        sigmoid_weight(1, 0, 1)
         rhs_half(1, 1)
-        pair(1, 0, 0)
-        sigmoid_weight(1, 0, 2)
-        sigmoid_weight(1, 0, 3)
-        rhs_half(2, 0)
-        pair(1, 0, 1)
+        pair(0, 0, 1)
+        interleave_left("V", 0, 1)
+        scale_all(0, 0, (0, 1))
+        quantize(("left", 0, 1))
         quantize(("rhs", 1, 0))
         quantize(("rhs", 1, 1))
-        quantize(("h", 0, 0))
-        interleave_right("S", 0, 0)
-        scale_all(1, 0)
+        sigmoid_weight(1, 0, 0)
+        sigmoid_weight(1, 0, 1)
+        rhs_half(2, 0)
+        scale_all(0, 0, (2,))
+        interleave_left("V", 1, 1)
+        scale_all(0, 0, (3,))
         pair(0, 1, 0)
+        sigmoid_weight(1, 0, 2)
+        sigmoid_weight(1, 0, 3)
         rhs_half(2, 1)
         pair(0, 1, 1)
-        interleave_right("S", 1, 0)
-        scale_all(0, 1, (0,))
-        quantize(("h", 0, 1))
-        scale_all(0, 1, (1,))
-        quantize(("right", 0, 0))
+        quantize(("left", 1, 1))
+        quantize(("h", 0, 0))
+        scale_all(0, 1, (0, 1))
+        products(1, 0)
         quantize(("rhs", 2, 0))
         quantize(("rhs", 2, 1))
+        shared_right(0, 0)
+        interleave_right("S", 1, 0)
         scale_all(0, 1, (2, 3))
-        interleave_right("S", 2, 0)
+        scale_all(1, 0, (0, 1))
         products(0, 2)
-        quantize(("right", 1, 0))
         quantize(("h", 1, 0))
+        quantize(("right", 1, 0))
+        quantize(("right", 0, 0))
+        whole("G", ("right", 2, 0), right_cols(2, 0))
         interleave_right("S", 0, 1)
+        interleave_right("S", 1, 1, "gstage2")
+        scale_all(1, 0, (2, 3))
+        wide(1, 1)
         scale_all(0, 2)
-        products(1, 1)
+        z_passes(0, 0, (0, 1))
+        scale_wide(1, 1)
         quantize(("right", 2, 0))
         quantize(("h", 2, 0))
-        interleave_right("S", 1, 1)
-        interleave_right("S", 2, 1)
-        scale_all(1, 1)
-        products_z(0, 0)
+        z_passes(0, 0, (2,))
+        quantize(("h", 0, 1))
         quantize(("right", 0, 1))
-        quantize(("h", 1, 1))
         quantize(("right", 1, 1))
-        interleave_right("S", 0, 2)
-        divide_all(0, 0)
         products(1, 2)
+        interleave_shared(("right", 2, 1), right_cols(2, 1), "gstage2")
+        whole("S", ("h", 1, 1), raw["h", 1, 1][:])
+        divide_all(0, 0)
         quantize(("right", 2, 1))
-        round_y("S", 0, 0, 0, W)
+        products_z(0, 1)
+        interleave_shared(("y", 0, 0), y32[0, 0][:], "gstage2")
         interleave_right("S", 1, 2)
         scale_all(1, 2)
-        products_z(0, 1)
-        quantize(("right", 0, 2))
+        quantize(("h", 1, 1))
         quantize(("h", 2, 1))
         quantize_y(0, 0)
-        interleave_right("S", 2, 2)
-        divide_all(0, 1)
         products_z(1, 0)
-        quantize(("right", 1, 2))
-        round_y("S", 0, 1, 0, W)
+        interleave_shared(("right", 0, 2), right_cols(0, 2), "gstage2")
         weights(1, 1)
-        divide_all(1, 0)
+        divide_all(0, 1)
         products_z(1, 1)
-        quantize(("right", 2, 2))
-        quantize_y(0, 1)
-        finish(1, 0, 256)
+        quantize(("right", 0, 2))
+        interleave_shared(("right", 2, 2), right_cols(2, 2), "gstage2")
         weights(0, 2)
-        divide_all(1, 1)
+        divide_all(1, 0)
+        quantize(("right", 1, 2))
+        quantize(("right", 2, 2))
         products_z(0, 2)
-        quantize_y(1, 0)
-        finish(1, 1, 256)
+        interleave_shared(("y", 0, 1), y32[0, 1][:], "gstage2")
+        round_y("S", 1, 0, 0, W)
+        divide_all(1, 1)
+        products_z(1, 2)
+        quantize_y(0, 1)
+        interleave_shared(("y", 1, 1), y32[1, 1][:], "gstage2")
         weights(1, 2)
         divide_all(0, 2)
-        products_z(1, 2)
+        quantize_y(1, 0)
         quantize_y(1, 1)
-        finish(0, 2, 128)
+        interleave_shared(("y", 0, 2), y32[0, 2][:], "gstage2")
         divide_all(1, 2)
         quantize_y(0, 2)
         finish(1, 2, 320)

@@ -108,12 +108,12 @@ def tile_sylvester_eigen_coordinates_h3_kernel(
             interleave("G", new_stage(key + ("G",), tag, G_COLS)[:], src[:, :, 0:G_COLS])
             interleave("S", new_stage(key + ("S",), "sstage", W - G_COLS)[:], src[:, :, G_COLS:W])
 
-        def quantize_into(key, codes_ap, scales_ap):
+        def quantize_into(key, codes_ap, scales_ap, order=1):
             if key in staged:
                 parts = [(key, slice(0, W))]
             else:
                 parts = [(key + ("S",), slice(G_COLS, W)), (key + ("G",), slice(0, G_COLS))]
-            for part, cols in parts:
+            for part, cols in parts[::order]:
                 nc.vector.quantize_mx(
                     out=codes_ap[:, cols].bitcast(FP8X4),
                     scales=scales_ap[:, cols],
@@ -219,14 +219,14 @@ def tile_sylvester_eigen_coordinates_h3_kernel(
                 scale=-1.0,
             )
 
-        def divide(g, lc, s):
-            if s == 0:
+        def divide(g, lc, s, cols=slice(0, W)):
+            if (g, lc) not in y32:
                 y32[g, lc] = shared.tile([P, PACK, W], F32, name="y32", tag="y32", bufs=Y_BUFS, offset=0)
             nc.vector.scalar_tensor_tensor(
-                out=y32[g, lc][:, s, :],
-                in0=banks["z", g, lc, s][:],
+                out=y32[g, lc][:, s, cols],
+                in0=banks["z", g, lc, s][:, cols],
                 scalar=inv_lam[:, PACK * g + s : PACK * g + s + 1],
-                in1=weight[g, lc][:, s, :],
+                in1=weight[g, lc][:, s, cols],
                 op0=ALU.mult,
                 op1=ALU.mult,
             )
@@ -235,15 +235,30 @@ def tile_sylvester_eigen_coordinates_h3_kernel(
             rows = out_0[g * KP : (g + 1) * KP, lc * W : (lc + 1) * W].rearrange("(p s) l -> p s l", s=PACK)
             nc.sync.dma_start(out=rows[:, s0:s1, :], in_=y32[g, lc][:, s0:s1, :])
 
+        def store_y_cols(g, lc, cols):
+            rows = out_0[g * KP : (g + 1) * KP, lc * W : (lc + 1) * W].rearrange("(p s) l -> p s l", s=PACK)
+            nc.sync.dma_start(out=rows[:, :, cols], in_=y32[g, lc][:, :, cols])
+
+        def quantize_y_half(g, lc, half):
+            cols = slice(lc * W + half * 256, lc * W + (half + 1) * 256)
+            y_codes = ring.tile([P, 256], U32, name="y_codes", tag="y_codes", bufs=6, align_bytes=64)
+            nc.vector.quantize_mx(
+                out=y_codes[:].bitcast(FP8X4),
+                scales=y_scales[PACK * g :, cols],
+                in_=staged["y", g, lc, half][:].rearrange("p w t -> p (w t)"),
+            )
+            dst = out_1[g].rearrange("p m t -> p (m t)").bitcast(I32)
+            nc.sync.dma_start(out=dst[:, cols], in_=y_codes[:].bitcast(I32))
+
         def round_y(engine, g, lc, lo, hi):
             if ("y", g, lc) not in staged:
                 new_stage(("y", g, lc))
             interleave(engine, staged["y", g, lc][:, lo:hi, :], y32[g, lc][:, :, lo:hi])
 
-        def quantize_y(g, lc):
+        def quantize_y(g, lc, order=1):
             cols = slice(lc * W, (lc + 1) * W)
             y_codes = ring.tile([P, W], U32, name="y_codes", tag="y_codes", bufs=6, align_bytes=64)
-            quantize_into(("y", g, lc), y_codes[:], y_scales[PACK * g :, cols])
+            quantize_into(("y", g, lc), y_codes[:], y_scales[PACK * g :, cols], order)
             dst = out_1[g].rearrange("p m t -> p (m t)").bitcast(I32)
             nc.sync.dma_start(out=dst[:, cols], in_=y_codes[:].bitcast(I32))
 
@@ -293,8 +308,8 @@ def tile_sylvester_eigen_coordinates_h3_kernel(
         load_left(1, 0)
         nc.sync.dma_start(out=rs[:], in_=row_scale.rearrange("(g p t) -> p g t", p=P, t=PACK))
         load_rhs(1, 0)
-        load_rhs(1, 1)
         load_left(0, 1)
+        load_rhs(1, 1)
         load_left(1, 1)
         load_rhs(2, 0)
         load_rhs(2, 1)
@@ -376,45 +391,46 @@ def tile_sylvester_eigen_coordinates_h3_kernel(
             for k in range(n):
                 mx_pass(bank[:], ("left", 0, 0), slice(0, P), ("left", 0, 0), slice(0, W), True, True)
 
-        for b in range(3):
-            spread_mu(b)
-            copy_mu("V", b)
         interleave_left("V", 0, 0)
-        sigmoid_weight(0, 0, 0)
-        sigmoid_weight(0, 0, 1)
+        spread_mu(0)
+        spread_mu(1)
+        spread_mu(2)
         rhs_half(0, 0)
         quantize(("left", 0, 0))
+        for b in range(3):
+            copy_mu("V", b)
         rhs_half(0, 1)
         interleave_left("V", 1, 0)
         quantize(("rhs", 0, 0))
         quantize(("rhs", 0, 1))
         quantize(("left", 1, 0))
+        sigmoid_weight(0, 0, 0)
+        sigmoid_weight(0, 0, 1)
         nc.vector.tensor_copy(out=rs32[:], in_=rs[:].rearrange("p g t -> p (g t)"))
         sigmoid_weight(0, 0, 2)
         sigmoid_weight(0, 0, 3)
-        sigmoid_weight(0, 1, 0)
-        sigmoid_weight(0, 1, 1)
-        warm_up(3)
+        warm_up(2)
         rhs_half(1, 0)
         pair(0, 0, 0)
-        sigmoid_weight(0, 1, 2)
-        sigmoid_weight(0, 1, 3)
+        sigmoid_weight(0, 1, 0)
+        sigmoid_weight(0, 1, 1)
         rhs_half(1, 1)
         pair(0, 0, 1)
         interleave_left("V", 0, 1)
-        scale_all(0, 0, (0, 1))
+        scale_all(0, 0, (0,))
         quantize(("left", 0, 1))
+        scale_all(0, 0, (1,))
+        interleave_left("V", 1, 1)
         quantize(("rhs", 1, 0))
         quantize(("rhs", 1, 1))
+        sigmoid_weight(0, 1, 2)
+        sigmoid_weight(0, 1, 3)
         sigmoid_weight(1, 0, 0)
-        sigmoid_weight(1, 0, 1)
         rhs_half(2, 0)
-        scale_all(0, 0, (2,))
-        interleave_left("V", 1, 1)
-        scale_all(0, 0, (3,))
+        scale_all(0, 0, (2, 3))
         pair(0, 1, 0)
+        sigmoid_weight(1, 0, 1)
         sigmoid_weight(1, 0, 2)
-        sigmoid_weight(1, 0, 3)
         rhs_half(2, 1)
         pair(0, 1, 1)
         quantize(("left", 1, 1))
@@ -448,6 +464,7 @@ def tile_sylvester_eigen_coordinates_h3_kernel(
         products(1, 2)
         interleave_shared(("right", 2, 1), right_cols(2, 1), "gstage2")
         whole("S", ("h", 1, 1), raw["h", 1, 1][:])
+        sigmoid_weight(1, 0, 3)
         divide_all(0, 0)
         quantize(("right", 2, 1))
         products_z(0, 1)
@@ -480,8 +497,17 @@ def tile_sylvester_eigen_coordinates_h3_kernel(
         quantize_y(1, 0)
         quantize_y(1, 1)
         interleave_shared(("y", 0, 2), y32[0, 2][:], "gstage2")
-        divide_all(1, 2)
+        first, second = slice(0, 256), slice(256, W)
+        for s in range(PACK):
+            divide(1, 2, s, first)
+        store_y_cols(1, 2, first)
+        interleave("S", new_stage(("y", 1, 2, "G"), "sstage", 256)[:], y32[1, 2][:, :, first])
+        for s in range(PACK):
+            divide(1, 2, s, second)
+        store_y_cols(1, 2, second)
         quantize_y(0, 2)
-        finish(1, 2, 320)
-        quantize_y(1, 2)
+        last = new_stage(("y", 1, 2, "S"), "stage", 256)
+        interleave("V", last[:, 0:160, :], y32[1, 2][:, :, 256:416])
+        interleave("S", last[:, 160:256, :], y32[1, 2][:, :, 416:W])
+        quantize_y(1, 2, -1)
         store_scales(0, 3, [nc.sync, nc.scalar, nc.sync, nc.scalar])

@@ -287,8 +287,6 @@ def tile_sylvester_eigen_coordinates_h3_kernel(
         lam_sb = keep.tile([P, A_GROUPS, PACK], BF16, name="lam_sb")
         rs = keep.tile([P, J_PASSES, PACK], BF16, name="rs")
         rs32 = keep.tile([P, J_PASSES * PACK], F32, name="rs32")
-        one = keep.tile([P, 1], F32, name="one")
-        warm = keep.tile([P, 2], F32, name="warm")
         ln_mu = keep.tile([P, MU_COLS], F32, name="ln_mu")
         ln_lam = keep.tile([P, A_GROUPS * PACK], F32, name="ln_lam")
         inv_lam = keep.tile([P, A_GROUPS * PACK], F32, name="inv_lam")
@@ -299,8 +297,6 @@ def tile_sylvester_eigen_coordinates_h3_kernel(
         nc.scalar.dma_start(out=mu_sb[:], in_=mu.rearrange("(n m) -> n m", m=MU_COLS))
         nc.scalar.dma_start(out=lam_sb[:], in_=lam.rearrange("(g p s) -> p g s", p=P, s=PACK))
         make_identity(nc, ident[:])
-        nc.vector.memset(one[:], 1.0)
-        nc.scalar.activation(out=warm[:, 0:1], in_=one[:], func=ACT.Ln)
 
         load_left(0, 0)
         load_rhs(0, 0)
@@ -320,7 +316,6 @@ def tile_sylvester_eigen_coordinates_h3_kernel(
 
         nc.scalar.activation(out=ln_mu[:], in_=mu_sb[:], func=ACT.Ln)
         nc.scalar.activation(out=ln_lam[:], in_=lam_sb[:].rearrange("p g s -> p (g s)"), func=ACT.Ln)
-        nc.scalar.activation(out=warm[:, 1:2], in_=one[:], func=ACT.Sigmoid)
         nc.vector.reciprocal(out=inv_lam[:], in_=lam_sb[:].rearrange("p g s -> p (g s)"))
 
         def rhs_half(jg, tp):
@@ -409,7 +404,6 @@ def tile_sylvester_eigen_coordinates_h3_kernel(
         nc.vector.tensor_copy(out=rs32[:], in_=rs[:].rearrange("p g t -> p (g t)"))
         sigmoid_weight(0, 0, 2)
         sigmoid_weight(0, 0, 3)
-        warm_up(2)
         rhs_half(1, 0)
         pair(0, 0, 0)
         sigmoid_weight(0, 1, 0)

from contextlib import ExitStack

import concourse.mybir as mybir
from concourse.masks import make_identity

NX, NY = 1024, 1536
FLOPS = 2 * NY * NX * NX + 2 * NX * NY * NY

F32 = mybir.dt.float32
BF16 = mybir.dt.bfloat16
I32 = mybir.dt.int32
U32 = mybir.dt.uint32
U8 = mybir.dt.uint8
FP8X4 = mybir.dt.float8_e4m3fn_x4
ACT = mybir.ActivationFunctionType
ALU = mybir.AluOpType

P = 128
PACK = 4
KP = P * PACK
W = 512
I_PASSES = NX // KP
J_PASSES = NY // KP
A_GROUPS = NX // KP
L_CHUNKS = NY // W
MU_COLS = NY // P
BUFS = {"stage": 6, "gstage": 1, "gstage2": 1, "sstage": 2}
WEIGHT_BUFS = 3
Y_BUFS = 4
G_COLS = 256


def tile_sylvester_eigen_coordinates_h3_kernel(
    tc, rhs, left, row_scale, right, lam, mu, out_0, out_1, out_2
):
    nc = tc.nc
    with ExitStack() as ctx:
        keep = ctx.enter_context(tc.tile_pool(name="keep", bufs=1))
        ring = ctx.enter_context(tc.tile_pool(name="ring", bufs=1))
        shared = ctx.enter_context(tc.tile_pool(name="shared", bufs=1))
        psum = ctx.enter_context(tc.psum_pool(name="psum", bufs=8))
        ctx.enter_context(tc.manual_schedule())

        raw = {}
        staged = {}
        banks = {}
        codes = {}
        scales = {}
        weight = {}
        y32 = {}

        def new_bank(key):
            banks[key] = psum.tile([P, W], F32, name="bank", tag="bank")
            return banks[key]

        def copy_on(engine, out, in_):
            if engine == "V":
                nc.vector.tensor_copy(out=out, in_=in_)
            else:
                nc.scalar.copy(out=out, in_=in_)

        def load_rows(key, src, width):
            raw[key] = keep.tile([P, PACK, width], BF16, name="raw_%s_%d_%d" % key)
            nc.sync.dma_start(out=raw[key][:], in_=src.rearrange("(p t) w -> p t w", t=PACK))

        def load_left(c, g):
            load_rows(("left", c, g), left[c * KP : (c + 1) * KP, g * W : (g + 1) * W], W)

        def load_right_first(c):
            load_rows(("right", c, 0), right[c * KP : (c + 1) * KP, 0:W], W)

        def load_right_rest(c):
            load_rows(("right", c, 1), right[c * KP : (c + 1) * KP, W:NY], NY - W)

        def load_rhs(jg, tp):
            raw["rhs", jg, tp] = shared.tile([P, 2, NX], BF16, name="rhs_raw", tag="rhs_raw", bufs=6, offset=0)
            rows = rhs[jg * KP : (jg + 1) * KP, :].rearrange("(m t) i -> m t i", t=PACK)
            nc.sync.dma_start(out=raw["rhs", jg, tp][:], in_=rows[:, 2 * tp : 2 * tp + 2, :])

        def new_stage(key, tag="stage", width=W):
            staged[key] = ring.tile([P, width, PACK], BF16, name=tag, tag=tag, bufs=BUFS[tag], align_bytes=64)
            return staged[key]

        def interleave(engine, dst, src):
            if engine == "G":
                nc.gpsimd.tensor_scalar(
                    out=dst, in0=src.rearrange("p t w -> p w t"), scalar1=1.0, scalar2=0.0, op0=ALU.mult, op1=ALU.add
                )
                return
            copy_on(
                engine,
                dst.rearrange("p (c i) t -> p c t i", i=4),
                src.rearrange("p t (c i) -> p c t i", i=4),
            )

        def interleave_left(engine, c, g):
            interleave(engine, new_stage(("left", c, g))[:], raw["left", c, g][:])

        def right_cols(c, lc):
            if lc == 0:
                return raw["right", c, 0][:]
            return raw["right", c, 1][:, :, (lc - 1) * W : lc * W]

        def interleave_right(engine, c, lc, tag="stage"):
            interleave(engine, new_stage(("right", c, lc), tag)[:], right_cols(c, lc))

        def interleave_shared(key, src, tag="gstage"):
            interleave("G", new_stage(key + ("G",), tag, G_COLS)[:], src[:, :, 0:G_COLS])
            interleave("S", new_stage(key + ("S",), "sstage", W - G_COLS)[:], src[:, :, G_COLS:W])

        def quantize_into(key, codes_ap, scales_ap, order=1):
            if key in staged:
                parts = [(key, slice(0, W))]
            else:
                parts = [(key + ("S",), slice(G_COLS, W)), (key + ("G",), slice(0, G_COLS))]
            for part, cols in parts[::order]:
                nc.vector.quantize_mx(
                    out=codes_ap[:, cols].bitcast(FP8X4),
                    scales=scales_ap[:, cols],
                    in_=staged[part][:].rearrange("p w t -> p (w t)"),
                )

        def quantize(key):
            codes[key] = keep.tile([P, W], U32, name="codes_%s_%d_%d" % key, align_bytes=64)
            scales[key] = keep.tile([P, W], U8, name="scales_%s_%d_%d" % key, align_bytes=64)
            quantize_into(key, codes[key][:], scales[key][:])

        def transpose_rhs(jg, c, tp):
            bank = new_bank(("rhs", jg, c, tp))
            for t2 in range(2):
                words = raw["rhs", jg, tp][:, t2, :].bitcast(F32)
                for u in range(2):
                    q = 2 * t2 + u
                    nc.tensor.transpose(
                        bank[:, q * P : (q + 1) * P], words[:, 256 * c + u : 256 * (c + 1) : 2], ident[:]
                    )

        def copy_rhs(engine, jg, c, tp):
            if (jg, c) == (2, 1):
                half = new_stage(("rhs", jg, c, "GS"[tp]), ("gstage", "sstage")[tp], 2 * P)[:]
            else:
                if tp == 0:
                    new_stage(("rhs", jg, c))
                half = staged["rhs", jg, c][:, tp * 2 * P : (tp + 1) * 2 * P, :]
            dst = half.rearrange("p w t -> p (w t)").bitcast(F32)
            copy_on(
                engine,
                dst.rearrange("p (t m u) -> p t m u", t=2, u=2),
                banks["rhs", jg, c, tp][:].rearrange("p (t u m) -> p t m u", t=2, u=2),
            )

        def mx_pass(out, stat, stat_cols, mov, mov_cols, start, stop):
            nc.tensor.matmul_mx(
                out=out,
                lhsT=codes[stat][:, stat_cols].bitcast(FP8X4),
                lhsT_scale=scales[stat][:, stat_cols],
                rhs=codes[mov][:, mov_cols].bitcast(FP8X4),
                rhs_scale=scales[mov][:, mov_cols],
                start=start,
                stop=stop,
            )

        def product_p(g, jg, b):
            bank = new_bank(("p", g, jg, b))
            for t in range(PACK):
                for c in range(I_PASSES):
                    mx_pass(
                        bank[:, t * P : (t + 1) * P],
                        ("rhs", jg, c), slice(t * P, (t + 1) * P),
                        ("left", c, g), slice(b * P, (b + 1) * P),
                        c == 0, c == I_PASSES - 1,
                    )

        def scale_rows(g, jg, b):
            if b == 0:
                new_stage(("h", jg, g))
            dst = staged["h", jg, g][:].rearrange("p (s m) t -> p s m t", s=PACK)[:, :, 32 * b : 32 * (b + 1), :]
            nc.vector.tensor_tensor(
                out=dst,
                in0=banks["p", g, jg, b][:].rearrange("p (t m s) -> p s m t", t=PACK, s=PACK),
                in1=rs[:, jg : jg + 1, :].unsqueeze(1).to_broadcast([P, PACK, 32, PACK]),
                op=ALU.mult,
            )

        def product_p_wide(g, jg, t):
            bank = new_bank(("pw", g, jg, t))
            for c in range(I_PASSES):
                mx_pass(
                    bank[:], ("rhs", jg, c), slice(t * P, (t + 1) * P), ("left", c, g), slice(0, W),
                    c == 0, c == I_PASSES - 1,
                )

        def scale_slot(g, jg, t):
            if t == 0:
                raw["h", jg, g] = ring.tile([P, PACK, W], BF16, name="h_rows", tag="h_rows", bufs=2)
            nc.scalar.activation(
                out=raw["h", jg, g][:, t, :].rearrange("p (s m) -> p s m", s=PACK),
                in_=banks["pw", g, jg, t][:].rearrange("p (m s) -> p s m", s=PACK),
                func=ACT.Copy,
                scale=rs32[:, PACK * jg + t : PACK * jg + t + 1],
            )

        def product_z(g, lc, s, passes=range(J_PASSES)):
            bank = new_bank(("z", g, lc, s)) if passes[0] == 0 else banks["z", g, lc, s]
            for c in passes:
                mx_pass(
                    bank[:], ("h", c, g), slice(s * P, (s + 1) * P), ("right", c, lc), slice(0, W),
                    c == 0, c == J_PASSES - 1,
                )

        def sigmoid_weight(g, lc, s):
            if s == 0:
                weight[g, lc] = ring.tile([P, PACK, W], F32, name="weight", tag="weight", bufs=WEIGHT_BUFS)
            nc.scalar.activation(
                out=weight[g, lc][:, s, :],
                in_=ln_mu_rows[lc][:],
                func=ACT.Sigmoid,
                bias=ln_lam[:, PACK * g + s : PACK * g + s + 1],
                scale=-1.0,
            )

        def divide(g, lc, s, cols=slice(0, W)):
            if (g, lc) not in y32:
                y32[g, lc] = shared.tile([P, PACK, W], F32, name="y32", tag="y32", bufs=Y_BUFS, offset=0)
            nc.vector.scalar_tensor_tensor(
                out=y32[g, lc][:, s, cols],
                in0=banks["z", g, lc, s][:, cols],
                scalar=inv_lam[:, PACK * g + s : PACK * g + s + 1],
                in1=weight[g, lc][:, s, cols],
                op0=ALU.mult,
                op1=ALU.mult,
            )

        def store_y(g, lc, s0, s1):
            rows = out_0[g * KP : (g + 1) * KP, lc * W : (lc + 1) * W].rearrange("(p s) l -> p s l", s=PACK)
            nc.sync.dma_start(out=rows[:, s0:s1, :], in_=y32[g, lc][:, s0:s1, :])

        def store_y_cols(g, lc, cols):
            rows = out_0[g * KP : (g + 1) * KP, lc * W : (lc + 1) * W].rearrange("(p s) l -> p s l", s=PACK)
            nc.sync.dma_start(out=rows[:, :, cols], in_=y32[g, lc][:, :, cols])

        def quantize_y_half(g, lc, half):
            cols = slice(lc * W + half * 256, lc * W + (half + 1) * 256)
            y_codes = ring.tile([P, 256], U32, name="y_codes", tag="y_codes", bufs=6, align_bytes=64)
            nc.vector.quantize_mx(
                out=y_codes[:].bitcast(FP8X4),
                scales=y_scales[PACK * g :, cols],
                in_=staged["y", g, lc, half][:].rearrange("p w t -> p (w t)"),
            )
            dst = out_1[g].rearrange("p m t -> p (m t)").bitcast(I32)
            nc.sync.dma_start(out=dst[:, cols], in_=y_codes[:].bitcast(I32))

        def round_y(engine, g, lc, lo, hi):
            if ("y", g, lc) not in staged:
                new_stage(("y", g, lc))
            interleave(engine, staged["y", g, lc][:, lo:hi, :], y32[g, lc][:, :, lo:hi])

        def quantize_y(g, lc, order=1):
            cols = slice(lc * W, (lc + 1) * W)
            y_codes = ring.tile([P, W], U32, name="y_codes", tag="y_codes", bufs=6, align_bytes=64)
            quantize_into(("y", g, lc), y_codes[:], y_scales[PACK * g :, cols], order)
            dst = out_1[g].rearrange("p m t -> p (m t)").bitcast(I32)
            nc.sync.dma_start(out=dst[:, cols], in_=y_codes[:].bitcast(I32))

        def store_scales(lc0, lc1, queues):
            cols = slice(lc0 * W, lc1 * W)
            for q in range(4):
                queues[q].dma_start(
                    out=out_2[:, 4 * q : 4 * q + 4, cols].bitcast(I32),
                    in_=y_scales[32 * q : 32 * q + 8, cols].bitcast(I32),
                )

        def spread_mu(b):
            bank = new_bank(("mu", b))
            for m in range(4):
                col = 4 * b + m
                nc.tensor.transpose(
                    bank[:, m * P : (m + 1) * P], ln_mu[:, col : col + 1].to_broadcast([P, P]), ident[:]
                )

        def copy_mu(engine, b):
            dst = ln_mu_all[:].rearrange("p (n m) -> p n m", m=MU_COLS)[:, :, 4 * b : 4 * b + 4]
            copy_on(engine, dst, banks["mu", b][:].rearrange("p (m n) -> p n m", m=4))

        ident = keep.tile([P, P], F32, name="ident")
        mu_sb = keep.tile([P, MU_COLS], BF16, name="mu_sb")
        lam_sb = keep.tile([P, A_GROUPS, PACK], BF16, name="lam_sb")
        rs = keep.tile([P, J_PASSES, PACK], BF16, name="rs")
        rs32 = keep.tile([P, J_PASSES * PACK], F32, name="rs32")
        ln_mu = keep.tile([P, MU_COLS], F32, name="ln_mu")
        ln_lam = keep.tile([P, A_GROUPS * PACK], F32, name="ln_lam")
        inv_lam = keep.tile([P, A_GROUPS * PACK], F32, name="inv_lam")
        ln_mu_all = keep.tile([P, NY], F32, name="ln_mu_all")
        ln_mu_rows = [ln_mu_all[:, lc * W : (lc + 1) * W] for lc in range(L_CHUNKS)]
        y_scales = keep.tile([P, NY], U8, name="y_scales", align_bytes=64)

        nc.scalar.dma_start(out=mu_sb[:], in_=mu.rearrange("(n m) -> n m", m=MU_COLS))
        nc.scalar.dma_start(out=lam_sb[:], in_=lam.rearrange("(g p s) -> p g s", p=P, s=PACK))
        make_identity(nc, ident[:])

        load_left(0, 0)
        load_rhs(0, 0)
        load_rhs(0, 1)
        load_left(1, 0)
        nc.sync.dma_start(out=rs[:], in_=row_scale.rearrange("(g p t) -> p g t", p=P, t=PACK))
        load_rhs(1, 0)
        load_left(0, 1)
        load_rhs(1, 1)
        load_left(1, 1)
        load_rhs(2, 0)
        load_rhs(2, 1)
        for c in range(J_PASSES):
            load_right_first(c)
        for c in range(J_PASSES):
            load_right_rest(c)

        nc.scalar.activation(out=ln_mu[:], in_=mu_sb[:], func=ACT.Ln)
        nc.scalar.activation(out=ln_lam[:], in_=lam_sb[:].rearrange("p g s -> p (g s)"), func=ACT.Ln)
        nc.vector.reciprocal(out=inv_lam[:], in_=lam_sb[:].rearrange("p g s -> p (g s)"))

        def rhs_half(jg, tp):
            for c in range(I_PASSES):
                transpose_rhs(jg, c, tp)
            for c in range(I_PASSES):
                copy_rhs("S", jg, c, tp)

        def weights(g, lc):
            for s in range(PACK):
                sigmoid_weight(g, lc, s)

        def stage1(g, jg, bs=range(4)):
            for b in bs:
                product_p(g, jg, b)
                scale_rows(g, jg, b)

        def products(g, jg):
            for b in range(4):
                product_p(g, jg, b)

        def scale_all(g, jg, bs=range(4)):
            for b in bs:
                scale_rows(g, jg, b)

        def products_z(g, lc):
            for s in range(PACK):
                product_z(g, lc, s)

        def divide_all(g, lc):
            for s in range(PACK):
                divide(g, lc, s)
                if s % 2:
                    store_y(g, lc, s - 1, s + 1)

        def finish(g, lc, split):
            round_y("V", g, lc, 0, split)
            round_y("S", g, lc, split, W)

        def pair(g, jg, half):
            for b in (2 * half, 2 * half + 1):
                product_p(g, jg, b)

        def shared_right(c, lc):
            interleave_shared(("right", c, lc), right_cols(c, lc))

        def shared_y(g, lc):
            interleave_shared(("y", g, lc), y32[g, lc][:])

        def wide(g, jg):
            for t in range(PACK):
                product_p_wide(g, jg, t)

        def scale_wide(g, jg):
            for t in range(PACK):
                scale_slot(g, jg, t)

        def z_passes(g, lc, passes):
            for c in passes:
                for s in range(PACK):
                    product_z(g, lc, s, range(c, c + 1))

        def whole(engine, key, src):
            interleave(engine, new_stage(key, "gstage" if engine == "G" else "stage")[:], src)

        def warm_up(n):
            bank = new_bank("warm")
            for k in range(n):
                mx_pass(bank[:], ("left", 0, 0), slice(0, P), ("left", 0, 0), slice(0, W), True, True)

        interleave_left("V", 0, 0)
        spread_mu(0)
        spread_mu(1)
        spread_mu(2)
        rhs_half(0, 0)
        quantize(("left", 0, 0))
        for b in range(3):
            copy_mu("V", b)
        rhs_half(0, 1)
        interleave_left("V", 1, 0)
        quantize(("rhs", 0, 0))
        quantize(("rhs", 0, 1))
        quantize(("left", 1, 0))
        sigmoid_weight(0, 0, 0)
        sigmoid_weight(0, 0, 1)
        nc.vector.tensor_copy(out=rs32[:], in_=rs[:].rearrange("p g t -> p (g t)"))
        sigmoid_weight(0, 0, 2)
        sigmoid_weight(0, 0, 3)
        rhs_half(1, 0)
        pair(0, 0, 0)
        sigmoid_weight(0, 1, 0)
        sigmoid_weight(0, 1, 1)
        rhs_half(1, 1)
        pair(0, 0, 1)
        interleave_left("V", 0, 1)
        scale_all(0, 0, (0,))
        quantize(("left", 0, 1))
        scale_all(0, 0, (1,))
        interleave_left("V", 1, 1)
        quantize(("rhs", 1, 0))
        quantize(("rhs", 1, 1))
        sigmoid_weight(0, 1, 2)
        sigmoid_weight(0, 1, 3)
        sigmoid_weight(1, 0, 0)
        rhs_half(2, 0)
        scale_all(0, 0, (2, 3))
        pair(0, 1, 0)
        sigmoid_weight(1, 0, 1)
        sigmoid_weight(1, 0, 2)
        rhs_half(2, 1)
        pair(0, 1, 1)
        quantize(("left", 1, 1))
        quantize(("h", 0, 0))
        scale_all(0, 1, (0, 1))
        products(1, 0)
        quantize(("rhs", 2, 0))
        quantize(("rhs", 2, 1))
        shared_right(0, 0)
        interleave_right("S", 1, 0)
        scale_all(0, 1, (2, 3))
        scale_all(1, 0, (0, 1))
        products(0, 2)
        quantize(("h", 1, 0))
        quantize(("right", 1, 0))
        quantize(("right", 0, 0))
        whole("G", ("right", 2, 0), right_cols(2, 0))
        interleave_right("S", 0, 1)
        interleave_right("S", 1, 1, "gstage2")
        scale_all(1, 0, (2, 3))
        wide(1, 1)
        scale_all(0, 2)
        z_passes(0, 0, (0, 1))
        scale_wide(1, 1)
        quantize(("right", 2, 0))
        quantize(("h", 2, 0))
        z_passes(0, 0, (2,))
        quantize(("h", 0, 1))
        quantize(("right", 0, 1))
        quantize(("right", 1, 1))
        products(1, 2)
        interleave_shared(("right", 2, 1), right_cols(2, 1), "gstage2")
        whole("S", ("h", 1, 1), raw["h", 1, 1][:])
        sigmoid_weight(1, 0, 3)
        divide_all(0, 0)
        quantize(("right", 2, 1))
        products_z(0, 1)
        interleave_shared(("y", 0, 0), y32[0, 0][:], "gstage2")
        interleave_right("S", 1, 2)
        scale_all(1, 2)
        quantize(("h", 1, 1))
        quantize(("h", 2, 1))
        quantize_y(0, 0)
        products_z(1, 0)
        interleave_shared(("right", 0, 2), right_cols(0, 2), "gstage2")
        weights(1, 1)
        divide_all(0, 1)
        products_z(1, 1)
        quantize(("right", 0, 2))
        interleave_shared(("right", 2, 2), right_cols(2, 2), "gstage2")
        weights(0, 2)
        divide_all(1, 0)
        quantize(("right", 1, 2))
        quantize(("right", 2, 2))
        products_z(0, 2)
        interleave_shared(("y", 0, 1), y32[0, 1][:], "gstage2")
        round_y("S", 1, 0, 0, W)
        divide_all(1, 1)
        products_z(1, 2)
        quantize_y(0, 1)
        interleave_shared(("y", 1, 1), y32[1, 1][:], "gstage2")
        weights(1, 2)
        divide_all(0, 2)
        quantize_y(1, 0)
        quantize_y(1, 1)
        interleave_shared(("y", 0, 2), y32[0, 2][:], "gstage2")
        first, second = slice(0, 256), slice(256, W)
        for s in range(PACK):
            divide(1, 2, s, first)
        store_y_cols(1, 2, first)
        interleave("S", new_stage(("y", 1, 2, "G"), "sstage", 256)[:], y32[1, 2][:, :, first])
        for s in range(PACK):
            divide(1, 2, s, second)
        store_y_cols(1, 2, second)
        quantize_y(0, 2)
        last = new_stage(("y", 1, 2, "S"), "stage", 256)
        interleave("V", last[:, 0:160, :], y32[1, 2][:, :, 256:416])
        interleave("S", last[:, 160:256, :], y32[1, 2][:, :, 416:W])
        quantize_y(1, 2, -1)
        store_scales(0, 3, [nc.sync, nc.scalar, nc.sync, nc.scalar])
